import numpy as np
import ml_dtypes


def mxq(x, axis, fmt="e4m3"):
    dtype, down = {"e4m3": (ml_dtypes.float8_e4m3fn, 7), "e5m2": (ml_dtypes.float8_e5m2, 14)}[fmt]
    v = np.moveaxis(np.asarray(x, np.float32).astype(ml_dtypes.bfloat16).astype(np.float64), axis, -1)
    blocks = v.reshape(v.shape[:-1] + (-1, 32))
    amax = np.abs(blocks).max(-1, keepdims=True)
    byte = np.maximum(np.where(amax > 0, np.frexp(amax)[1] - 1 + 127, 0) - down, 1)
    scale = np.exp2(byte - 127.0)
    codes = (blocks / scale).astype(np.float32).astype(dtype).astype(np.float64)
    return np.moveaxis((codes * scale).reshape(v.shape), -1, axis)


WIDE = False


def mx_kscale(k):
    if not WIDE:
        return np.ones(k)
    levels = np.array([10, -10, 5, -5, 0])
    if k % 512:
        return np.exp2(np.random.permutation(np.resize(levels, k // 32))).repeat(32)
    a = np.empty((k // 512, 16))
    for p in range(k // 512):
        a[p, :8] = np.random.permutation(np.resize(levels, 8))
        for g in range(8):
            far = levels[np.abs(levels - a[p, g]) >= 10]
            a[p, g + 8] = far[np.random.randint(len(far))]
    return np.exp2(a.ravel()).repeat(32)


def f64(x):
    return np.asarray(x).astype(np.float64)


def striped(idx):
    return np.tile(idx.reshape(-1, 16).T, (8, 1)).astype(np.uint16)


def unstriped(offs):
    return offs[:16].T.reshape(-1).astype(np.int64)


def pack_weight(w):
    k, n = w.shape
    w = f64(np.asarray(w, np.float32).astype(ml_dtypes.bfloat16)).reshape(k // 32, 32, n)
    amax = np.abs(w).max(1)
    byte = np.clip(np.where(amax > 0, np.frexp(amax)[1] - 1 + 127 - 7, 1), 1, 254)
    scaled = (w * np.exp2(127.0 - byte)[:, None, :]).reshape(k, n).astype(np.float32)
    words = np.ascontiguousarray(scaled.reshape(k // 512, 128, 4, n).transpose(0, 1, 3, 2)).astype(ml_dtypes.float8_e4m3fn).view(np.uint8)
    return words, np.ascontiguousarray(byte.astype(np.uint8).reshape(k // 512, 16, n))


def unpack_weight(words, scales):
    g, p, n, _ = words.shape
    vals = np.ascontiguousarray(words).view(ml_dtypes.float8_e4m3fn).astype(np.float64) * np.repeat(np.exp2(scales.astype(np.float64) - 127.0), 8, axis=1)[..., None]
    return vals.transpose(0, 1, 3, 2).reshape(g * 512, n)


K, T, S, N = 512, 1024, 512, 128
P = 2 ** 7


def setup_inputs():
    n = np.random.standard_normal
    s = mx_kscale(K)[:, None]
    packed_xT = pack_weight(n((K, T)) * s)
    return {
        "x_words": packed_xT[0],
        "x_scales": packed_xT[1],
        "w1": (n((K, N)) / np.sqrt(K) / s).astype(np.float32),
        "w2": (n((K, N)) / np.sqrt(K) / s).astype(np.float32),
        "mu": (n((N, S)) * 0.5).astype(np.float32),
        "cap": (np.tile(np.random.uniform(0.8, 1.5, S), (P, 1))).astype(np.float32),
        "rew": (np.tile(n(S), (P, 1))).astype(np.float32),
        "gam": (np.tile(np.random.uniform(0.6, 0.99, S) * (np.random.uniform(size=S) < 0.95), (P, 1))).astype(np.float32),
        "offs": striped(np.random.permutation(T)[:S]),
    }


def reference(x_words, x_scales, w1, w2, mu, cap, rew, gam, offs):
    xq = unpack_weight(x_words, x_scales)[:, unstriped(offs)]
    val = mxq(f64(w2), 0, "e4m3").T @ xq
    yl = mxq(f64(w1), 0, "e4m3").T @ xq
    ratio = np.minimum(np.exp(yl - f64(mu)), f64(cap)[:1])
    dlt = ratio * (f64(rew)[:1] + f64(gam)[:1] * (np.pad(val, ((0, 0), (0, 1)))[:, 1:]) - val)
    gc = f64(gam)[:1] * ratio
    sa = dlt + gc * (np.pad(dlt, ((0, 0), (0, 1)))[:, 1:])
    cc2 = gc * (np.pad(gc, ((0, 0), (0, 1)))[:, 1:])
    return val + sa + cc2 * (np.pad(sa, ((0, 0), (0, 2)))[:, 2:])

@@ -1,0 +1,127 @@
+from contextlib import ExitStack
+
+import concourse.mybir as mybir
+
+K, T, S, M = 512, 1024, 512, 128
+FLOPS = 2 * 2 * K * M * S
+
+F32 = mybir.dt.float32
+BF16 = mybir.dt.bfloat16
+I32 = mybir.dt.int32
+U32 = mybir.dt.uint32
+U16 = mybir.dt.uint16
+U8 = mybir.dt.uint8
+FP8X4 = mybir.dt.float8_e4m3fn_x4
+ALU = mybir.AluOpType
+ACT = mybir.ActivationFunctionType
+
+P = 128
+HALF = S // 2
+
+
+def tile_picked_yvtrac_tgt_p_kernel(tc, x_words, x_scales, w1, w2, mu, cap, rew, gam, offs, out):
+    nc = tc.nc
+    with ExitStack() as ctx:
+        keep = ctx.enter_context(tc.tile_pool(name="keep", bufs=1))
+        psum = ctx.enter_context(tc.psum_pool(name="psum", bufs=1))
+
+        offsets = keep.tile([P, S // 16], U16, name="offsets")
+        nc.sync.dma_start(offsets[:], offs)
+
+        table_scales = keep.tile([P, T], U8, name="table_scales", align_bytes=64)
+        nc.vector.memset(table_scales[:].bitcast(I32), 0)
+        for q in range(4):
+            nc.scalar.dma_start(out=table_scales[32 * q : 32 * q + 4, :].bitcast(I32), in_=x_scales[0, 4 * q : 4 * q + 4, :].bitcast(I32))
+
+        table_words = keep.tile([P, T], U32, name="table_words", align_bytes=64)
+        nc.sync.dma_start(out=table_words[:].bitcast(I32), in_=x_words[0].rearrange("p c r -> p (c r)").bitcast(I32))
+
+        def load(name, src, shape):
+            t = keep.tile(shape, F32, name=name)
+            nc.sync.dma_start(out=t[:], in_=src)
+            return t
+
+        w1_raw = load("w1_raw", w1.rearrange("(p j) m -> p j m", j=4), [P, 4, M])
+        w2_raw = load("w2_raw", w2.rearrange("(p j) m -> p j m", j=4), [P, 4, M])
+        mu_sb = load("mu_sb", mu, [P, S])
+        gam_sb = load("gam_sb", gam, [P, S])
+        rew_sb = load("rew_sb", rew, [P, S])
+        cap_sb = load("cap_sb", cap, [P, S])
+
+        halves = [slice(HALF, S), slice(0, HALF)]
+
+        picked_scales = keep.tile([P, S], U8, name="picked_scales", align_bytes=64)
+        nc.vector.tensor_copy(picked_scales[:], table_scales[:].indirect(offsets[:]))
+        picked_words = []
+        for h, cols in enumerate(halves):
+            t = keep.tile([P, HALF], U32, name="picked_words%d" % h, align_bytes=64)
+            nc.vector.tensor_copy(t[:], table_words[:].indirect(offsets[:, cols.start // 16 : cols.stop // 16]))
+            picked_words.append(t)
+
+        def quantise(name, raw):
+            grouped = keep.tile([P, M, 4], BF16, name=name + "_grouped", align_bytes=64)
+            nc.scalar.activation(out=grouped[:], in_=raw[:].rearrange("p j m -> p m j"), func=ACT.Copy)
+            codes = keep.tile([P, M], U32, name=name + "_codes", align_bytes=64)
+            scales = keep.tile([P, M], U8, name=name + "_scales", align_bytes=64)
+            nc.vector.quantize_mx(out=codes[:].bitcast(FP8X4), scales=scales[:], in_=grouped[:].rearrange("p m j -> p (m j)"))
+            return codes, scales
+
+        w1_codes, w1_scales = quantise("w1", w1_raw)
+        w2_codes, w2_scales = quantise("w2", w2_raw)
+
+        yl = []
+        for h, cols in enumerate(halves):
+            bank = psum.tile([P, HALF], F32, name="yl%d" % h)
+            nc.tensor.matmul_mx(out=bank[:], lhsT=w1_codes[:].bitcast(FP8X4), lhsT_scale=w1_scales[:],
+                                rhs=picked_words[h][:].bitcast(FP8X4), rhs_scale=picked_scales[:, cols], start=True, stop=True)
+            yl.append(bank)
+        val = psum.tile([P, S], F32, name="val")
+        for h, cols in enumerate(halves):
+            nc.tensor.matmul_mx(out=val[:, cols], lhsT=w2_codes[:].bitcast(FP8X4), lhsT_scale=w2_scales[:],
+                                rhs=picked_words[h][:].bitcast(FP8X4), rhs_scale=picked_scales[:, cols], start=True, stop=True)
+
+        def row(name, pad=0):
+            t = keep.tile([P, S + pad], F32, name=name)
+            if pad:
+                nc.gpsimd.memset(t[:, S:], 0.0)
+            return t
+
+        def shifted(cols, by):
+            return slice(cols.start + by, cols.stop + by)
+
+        diff, ex, ratio, back, td = row("diff"), row("ex"), row("ratio"), row("back"), row("td")
+        nxt = keep.tile([P, S], F32, name="nxt")
+        nc.vector.memset(nxt[:, S - 1 :], 0.0)
+        dlt, gc, sa = row("dlt", 1), row("gc", 1), row("sa", 2)
+        u, cc2, w, o, res = row("u"), row("cc2"), row("w"), row("o"), row("res")
+
+        tt = nc.vector.tensor_tensor
+        for h, c in enumerate(halves):
+            tt(diff[:, c], yl[h][:], mu_sb[:, c], ALU.subtract)
+            nc.scalar.activation(out=ex[:, c], in_=diff[:, c], func=ACT.Exp)
+        for c in halves:
+            stop = min(c.stop, S - 1)
+            tt(nxt[:, c.start : stop], val[:, c.start + 1 : stop + 1], gam_sb[:, c.start : stop], ALU.mult)
+        for c in halves:
+            tt(back[:, c], rew_sb[:, c], val[:, c], ALU.subtract)
+        for c in halves:
+            tt(ratio[:, c], ex[:, c], cap_sb[:, c], ALU.min)
+        for c in halves:
+            tt(td[:, c], nxt[:, c], back[:, c], ALU.add)
+        for c in halves:
+            tt(gc[:, c], ratio[:, c], gam_sb[:, c], ALU.mult)
+        for c in halves:
+            tt(dlt[:, c], ratio[:, c], td[:, c], ALU.mult)
+        for c in halves:
+            tt(u[:, c], gc[:, c], dlt[:, shifted(c, 1)], ALU.mult)
+        for c in halves:
+            tt(sa[:, c], dlt[:, c], u[:, c], ALU.add)
+        for c in halves:
+            tt(cc2[:, c], gc[:, c], gc[:, shifted(c, 1)], ALU.mult)
+        for c in halves:
+            tt(w[:, c], cc2[:, c], sa[:, shifted(c, 2)], ALU.mult)
+        for c in halves:
+            tt(o[:, c], val[:, c], sa[:, c], ALU.add)
+        for c in halves:
+            tt(res[:, c], o[:, c], w[:, c], ALU.add)
+            nc.sync.dma_start(out=out[:, c], in_=res[:, c])

@@ -17,6 +17,7 @@ ACT = mybir.ActivationFunctionType
 
 P = 128
 HALF = S // 2
+CHUNKS = S // P
 
 
 def tile_picked_yvtrac_tgt_p_kernel(tc, x_words, x_scales, w1, w2, mu, cap, rew, gam, offs, out):
@@ -29,12 +30,10 @@ def tile_picked_yvtrac_tgt_p_kernel(tc, x_words, x_scales, w1, w2, mu, cap, rew,
         nc.sync.dma_start(offsets[:], offs)
 
         table_scales = keep.tile([P, T], U8, name="table_scales", align_bytes=64)
-        nc.vector.memset(table_scales[:].bitcast(I32), 0)
         for q in range(4):
-            nc.scalar.dma_start(out=table_scales[32 * q : 32 * q + 4, :].bitcast(I32), in_=x_scales[0, 4 * q : 4 * q + 4, :].bitcast(I32))
-
-        table_words = keep.tile([P, T], U32, name="table_words", align_bytes=64)
-        nc.sync.dma_start(out=table_words[:].bitcast(I32), in_=x_words[0].rearrange("p c r -> p (c r)").bitcast(I32))
+            queue = nc.sync if q < 2 else nc.scalar
+            four_rows = x_scales[0, 4 * q : 4 * q + 4, :].bitcast(I32)
+            queue.dma_start(out=table_scales[32 * q : 32 * q + 32, :].bitcast(I32), in_=four_rows.unsqueeze(0).to_broadcast([8, 4, T // 4]))
 
         def load(name, src, shape):
             t = keep.tile(shape, F32, name=name)
@@ -42,43 +41,31 @@ def tile_picked_yvtrac_tgt_p_kernel(tc, x_words, x_scales, w1, w2, mu, cap, rew,
             return t
 
         w1_raw = load("w1_raw", w1.rearrange("(p j) m -> p j m", j=4), [P, 4, M])
+        table_words = keep.tile([P, T], U32, name="table_words", align_bytes=64)
+        nc.sync.dma_start(out=table_words[:].bitcast(I32), in_=x_words[0].rearrange("p c r -> p (c r)").bitcast(I32))
         w2_raw = load("w2_raw", w2.rearrange("(p j) m -> p j m", j=4), [P, 4, M])
+
+        ident = keep.tile([P, P], F32, name="ident")
+        nc.vector.memset(ident[:], 0.0)
+        ones = keep.tile([P, 32], F32, name="ones")
+        nc.vector.memset(ones[:], 1.0)
+        ramp = keep.tile([P, 32], F32, name="ramp", align_bytes=64)
+        nc.vector.tensor_tensor_scan(ramp[:], ones[:], ones[:], 0.0, ALU.mult, ALU.add)
+        ramp_t = keep.tile([P, 32], F32, name="ramp_t", align_bytes=64)
+        nc.vector.transpose(ramp_t[:], ramp[:])
+        for q in range(4):
+            quad = slice(32 * q, 32 * q + 32)
+            nc.vector.tensor_tensor(ident[quad, quad], ramp[quad, :], ramp_t[quad, :], ALU.is_equal)
+
+        rows = keep.tile([P, P], F32, name="rows")
+        nc.gpsimd.memset(rows[:], 0.0)
+        before_high = S - 1 + HALF
+        nc.sync.dma_start(out=rows[2:5, :], in_=rew.rearrange("r j -> (r j)")[before_high : before_high + 3 * P].rearrange("(c n) -> c n", n=P))
+        nc.sync.dma_start(out=rows[0:2, :], in_=gam.rearrange("r j -> (r j)")[before_high : before_high + 2 * P].rearrange("(c n) -> c n", n=P))
         mu_sb = load("mu_sb", mu, [P, S])
-        gam_sb = load("gam_sb", gam, [P, S])
-        rew_sb = load("rew_sb", rew, [P, S])
+        rew_low = load("rew_low", rew[:, 0 : HALF + 3], [P, HALF + 3])
         cap_sb = load("cap_sb", cap, [P, S])
-
-        halves = [slice(HALF, S), slice(0, HALF)]
-
-        picked_scales = keep.tile([P, S], U8, name="picked_scales", align_bytes=64)
-        nc.vector.tensor_copy(picked_scales[:], table_scales[:].indirect(offsets[:]))
-        picked_words = []
-        for h, cols in enumerate(halves):
-            t = keep.tile([P, HALF], U32, name="picked_words%d" % h, align_bytes=64)
-            nc.vector.tensor_copy(t[:], table_words[:].indirect(offsets[:, cols.start // 16 : cols.stop // 16]))
-            picked_words.append(t)
-
-        def quantise(name, raw):
-            grouped = keep.tile([P, M, 4], BF16, name=name + "_grouped", align_bytes=64)
-            nc.scalar.activation(out=grouped[:], in_=raw[:].rearrange("p j m -> p m j"), func=ACT.Copy)
-            codes = keep.tile([P, M], U32, name=name + "_codes", align_bytes=64)
-            scales = keep.tile([P, M], U8, name=name + "_scales", align_bytes=64)
-            nc.vector.quantize_mx(out=codes[:].bitcast(FP8X4), scales=scales[:], in_=grouped[:].rearrange("p m j -> p (m j)"))
-            return codes, scales
-
-        w1_codes, w1_scales = quantise("w1", w1_raw)
-        w2_codes, w2_scales = quantise("w2", w2_raw)
-
-        yl = []
-        for h, cols in enumerate(halves):
-            bank = psum.tile([P, HALF], F32, name="yl%d" % h)
-            nc.tensor.matmul_mx(out=bank[:], lhsT=w1_codes[:].bitcast(FP8X4), lhsT_scale=w1_scales[:],
-                                rhs=picked_words[h][:].bitcast(FP8X4), rhs_scale=picked_scales[:, cols], start=True, stop=True)
-            yl.append(bank)
-        val = psum.tile([P, S], F32, name="val")
-        for h, cols in enumerate(halves):
-            nc.tensor.matmul_mx(out=val[:, cols], lhsT=w2_codes[:].bitcast(FP8X4), lhsT_scale=w2_scales[:],
-                                rhs=picked_words[h][:].bitcast(FP8X4), rhs_scale=picked_scales[:, cols], start=True, stop=True)
+        gam_sb = load("gam_sb", gam, [P, S])
 
         def row(name, pad=0):
             t = keep.tile([P, S + pad], F32, name=name)
@@ -86,42 +73,104 @@ def tile_picked_yvtrac_tgt_p_kernel(tc, x_words, x_scales, w1, w2, mu, cap, rew,
                 nc.gpsimd.memset(t[:, S:], 0.0)
             return t
 
-        def shifted(cols, by):
-            return slice(cols.start + by, cols.stop + by)
-
-        diff, ex, ratio, back, td = row("diff"), row("ex"), row("ratio"), row("back"), row("td")
-        nxt = keep.tile([P, S], F32, name="nxt")
-        nc.vector.memset(nxt[:, S - 1 :], 0.0)
-        dlt, gc, sa = row("dlt", 1), row("gc", 1), row("sa", 2)
+        ex, ratio = row("ex"), row("ratio")
+        gc, sa = row("gc", 1), row("sa", 2)
+        dlt = keep.tile([P, S + 1], F32, name="dlt")
+        nc.scalar.activation(out=dlt[:, S:], in_=gc[:, S:], func=ACT.Copy)
         u, cc2, w, o, res = row("u"), row("cc2"), row("w"), row("o"), row("res")
 
+        def turn(dst, src, start, stop):
+            nc.tensor.matmul(dst, lhsT=src, rhs=ident[:], is_transpose=True, start=start, stop=stop)
+
+        picked_scales = keep.tile([P, S], U8, name="picked_scales", align_bytes=64)
+        nc.vector.tensor_copy(picked_scales[:], table_scales[:].indirect(offsets[:]))
+
+        def quantise(name, raw):
+            grouped = keep.tile([P, M, 4], BF16, name=name + "_grouped", tag=name + "_grouped", align_bytes=64)
+            nc.scalar.activation(out=grouped[:], in_=raw[:].rearrange("p j m -> p m j"), func=ACT.Copy)
+            codes = keep.tile([P, M], U32, name=name + "_codes", align_bytes=64)
+            scales = keep.tile([P, M], U8, name=name + "_scales", align_bytes=64)
+            nc.vector.quantize_mx(out=codes[:].bitcast(FP8X4), scales=scales[:], in_=grouped[:].rearrange("p m j -> p (m j)"))
+            return codes, scales
+
+        w1_codes, w1_scales = quantise("w1", w1_raw)
+
+        picked_words = [keep.tile([P, HALF], U32, name="picked_words%d" % h, align_bytes=64) for h in range(2)]
+
+        def words_of(c, n=P):
+            return picked_words[c // 2][:, (c % 2) * P : (c % 2) * P + n]
+
+        yl = []
+        for c in range(CHUNKS):
+            nc.vector.tensor_copy(words_of(c), table_words[:].indirect(offsets[:, c * P // 16 : (c + 1) * P // 16]))
+            bank = psum.tile([P, P], F32, name="yl%d" % c)
+            nc.tensor.matmul_mx(out=bank[:], lhsT=w1_codes[:].bitcast(FP8X4), lhsT_scale=w1_scales[:],
+                                rhs=words_of(c).bitcast(FP8X4), rhs_scale=picked_scales[:, c * P : (c + 1) * P], start=True, stop=True)
+            yl.append(bank)
+
+        w2_codes, w2_scales = quantise("w2", w2_raw)
+
+        val_low = psum.tile([P, HALF + 64], F32, name="val_low")
+        nc.tensor.matmul_mx(out=val_low[:, 0:HALF], lhsT=w2_codes[:].bitcast(FP8X4), lhsT_scale=w2_scales[:],
+                            rhs=picked_words[0][:].bitcast(FP8X4), rhs_scale=picked_scales[:, 0:HALF], start=True, stop=True)
+        nc.tensor.matmul_mx(out=val_low[:, HALF : HALF + 64], lhsT=w2_codes[:].bitcast(FP8X4), lhsT_scale=w2_scales[:],
+                            rhs=words_of(2, 64).bitcast(FP8X4), rhs_scale=picked_scales[:, HALF : HALF + 64], start=True, stop=True)
+        val_t = psum.tile([P, 2, M], F32, name="val_t")
+        for i in range(2):
+            c = 2 + i
+            nc.tensor.matmul_mx(out=val_t[:, i, :], lhsT=words_of(c).bitcast(FP8X4), lhsT_scale=picked_scales[:, c * P : (c + 1) * P],
+                                rhs=w2_codes[:].bitcast(FP8X4), rhs_scale=w2_scales[:], start=True, stop=True)
+
         tt = nc.vector.tensor_tensor
-        for h, c in enumerate(halves):
-            tt(diff[:, c], yl[h][:], mu_sb[:, c], ALU.subtract)
-            nc.scalar.activation(out=ex[:, c], in_=diff[:, c], func=ACT.Exp)
-        for c in halves:
-            stop = min(c.stop, S - 1)
-            tt(nxt[:, c.start : stop], val[:, c.start + 1 : stop + 1], gam_sb[:, c.start : stop], ALU.mult)
-        for c in halves:
-            tt(back[:, c], rew_sb[:, c], val[:, c], ALU.subtract)
-        for c in halves:
-            tt(ratio[:, c], ex[:, c], cap_sb[:, c], ALU.min)
-        for c in halves:
-            tt(td[:, c], nxt[:, c], back[:, c], ALU.add)
-        for c in halves:
-            tt(gc[:, c], ratio[:, c], gam_sb[:, c], ALU.mult)
-        for c in halves:
-            tt(dlt[:, c], ratio[:, c], td[:, c], ALU.mult)
-        for c in halves:
-            tt(u[:, c], gc[:, c], dlt[:, shifted(c, 1)], ALU.mult)
-        for c in halves:
-            tt(sa[:, c], dlt[:, c], u[:, c], ALU.add)
-        for c in halves:
-            tt(cc2[:, c], gc[:, c], gc[:, shifted(c, 1)], ALU.mult)
-        for c in halves:
-            tt(w[:, c], cc2[:, c], sa[:, shifted(c, 2)], ALU.mult)
-        for c in halves:
-            tt(o[:, c], val[:, c], sa[:, c], ALU.add)
-        for c in halves:
-            tt(res[:, c], o[:, c], w[:, c], ALU.add)
-            nc.sync.dma_start(out=out[:, c], in_=res[:, c])
+        for c in range(CHUNKS):
+            cols = slice(c * P, (c + 1) * P)
+            diff = keep.tile([P, P], F32, name="diff%d" % c, tag="diff%d" % c)
+            tt(diff[:], yl[c][:], mu_sb[:, cols], ALU.subtract)
+            nc.scalar.activation(out=ex[:, cols], in_=diff[:], func=ACT.Exp)
+
+        rows_t = psum.tile([P, P], F32, name="rows_t", tag="rows_then_td")
+        nc.tensor.transpose(rows_t[:], rows[:], ident[:])
+        consts = keep.tile([P, 5], F32, name="consts", tag="diff2")
+        nc.scalar.activation(out=consts[:], in_=rows_t[:, 0:5], func=ACT.Copy)
+
+        td = psum.tile([P, 3 * P], F32, name="td", tag="rows_then_td")
+        turn(td[:, 2 * P : 3 * P], consts[:, 4:5].to_broadcast([P, M]), True, False)
+        for i in range(2):
+            ahead = keep.tile([P, M], F32, name="ahead%d" % i)
+            nc.scalar.activation(out=ahead[:], in_=val_t[:, i, :], func=ACT.Identity, scale=consts[:, i : i + 1], bias=consts[:, 2 + i : 3 + i])
+            turn(td[:, i * P : (i + 1) * P], ahead[:], False, False)
+        minus = keep.tile([P, 2, M], F32, name="minus", tag="diff3")
+        nc.scalar.activation(out=minus[:], in_=val_t[:], func=ACT.Copy, scale=-1.0)
+        for i in range(2):
+            turn(td[:, i * P + 1 : (i + 1) * P + 1], minus[:, i, :], False, i == 1)
+        minus_val = psum.tile([P, HALF], F32, name="minus_val")
+        for i in range(2):
+            turn(minus_val[:, i * P : (i + 1) * P], minus[:, i, :], True, True)
+
+        back = keep.tile([P, HALF + 3], F32, name="back")
+        nxt = keep.tile([P, HALF + 3], F32, name="nxt")
+        td_low = keep.tile([P, HALF + 3], F32, name="td_low")
+
+        def part(t, h, reach=0, by=0):
+            return t[:, by : HALF + reach + by] if h == 0 else t[:, HALF + reach + by : S + by]
+
+        steps = {
+            "back": lambda h: tt(back[:], rew_low[:], val_low[:, 0 : HALF + 3], ALU.subtract),
+            "nxt": lambda h: tt(nxt[:], val_low[:, 1 : HALF + 4], gam_sb[:, 0 : HALF + 3], ALU.mult),
+            "td": lambda h: tt(td_low[:], nxt[:], back[:], ALU.add),
+            "ratio": lambda h: tt(part(ratio, h), part(ex, h), part(cap_sb, h), ALU.min),
+            "gc": lambda h: tt(part(gc, h), part(ratio, h), part(gam_sb, h), ALU.mult),
+            "cc2": lambda h: tt(part(cc2, h), part(gc, h), part(gc, h, 0, 1), ALU.mult),
+            "dlt": lambda h: tt(part(dlt, h, 3), td[:, 4 : HALF + 1] if h else td_low[:], part(ratio, h, 3), ALU.mult),
+            "u": lambda h: tt(part(u, h, 2), part(gc, h, 2), part(dlt, h, 2, 1), ALU.mult),
+            "sa": lambda h: tt(part(sa, h, 2), part(dlt, h, 2), part(u, h, 2), ALU.add),
+            "w": lambda h: tt(part(w, h), part(cc2, h), part(sa, h, 0, 2), ALU.mult),
+            "o": lambda h: tt(part(o, h), part(sa, h), minus_val[:] if h else val_low[:, 0:HALF], ALU.subtract if h else ALU.add),
+            "res": lambda h: tt(part(res, h), part(o, h), part(w, h), ALU.add),
+        }
+        order = [("back", 0), ("ratio", 0), ("ratio", 1), ("nxt", 0), ("gc", 0), ("td", 0), ("gc", 1), ("dlt", 0), ("cc2", 0), ("u", 0),
+                 ("dlt", 1), ("sa", 0), ("u", 1), ("w", 0), ("sa", 1), ("o", 0), ("cc2", 1), ("o", 1), ("w", 1), ("res", 0), ("res", 1)]
+        for name, h in order:
+            steps[name](h)
+            if name == "res":
+                nc.sync.dma_start(out=part(out, h), in_=part(res, h))

from contextlib import ExitStack

import concourse.mybir as mybir

K, T, S, M = 512, 1024, 512, 128
FLOPS = 2 * 2 * K * M * S

F32 = mybir.dt.float32
BF16 = mybir.dt.bfloat16
I32 = mybir.dt.int32
U32 = mybir.dt.uint32
U16 = mybir.dt.uint16
U8 = mybir.dt.uint8
FP8X4 = mybir.dt.float8_e4m3fn_x4
ALU = mybir.AluOpType
ACT = mybir.ActivationFunctionType

P = 128
HALF = S // 2
CHUNKS = S // P


def tile_picked_yvtrac_tgt_p_kernel(tc, x_words, x_scales, w1, w2, mu, cap, rew, gam, offs, out):
    nc = tc.nc
    with ExitStack() as ctx:
        keep = ctx.enter_context(tc.tile_pool(name="keep", bufs=1))
        psum = ctx.enter_context(tc.psum_pool(name="psum", bufs=1))

        offsets = keep.tile([P, S // 16], U16, name="offsets")
        nc.sync.dma_start(offsets[:], offs)

        table_scales = keep.tile([P, T], U8, name="table_scales", align_bytes=64)
        for q in range(4):
            queue = nc.sync if q < 2 else nc.scalar
            four_rows = x_scales[0, 4 * q : 4 * q + 4, :].bitcast(I32)
            queue.dma_start(out=table_scales[32 * q : 32 * q + 32, :].bitcast(I32), in_=four_rows.unsqueeze(0).to_broadcast([8, 4, T // 4]))

        def load(name, src, shape):
            t = keep.tile(shape, F32, name=name)
            nc.sync.dma_start(out=t[:], in_=src)
            return t

        w1_raw = load("w1_raw", w1.rearrange("(p j) m -> p j m", j=4), [P, 4, M])
        table_words = keep.tile([P, T], U32, name="table_words", align_bytes=64)
        nc.sync.dma_start(out=table_words[:].bitcast(I32), in_=x_words[0].rearrange("p c r -> p (c r)").bitcast(I32))
        w2_raw = load("w2_raw", w2.rearrange("(p j) m -> p j m", j=4), [P, 4, M])

        ident = keep.tile([P, P], F32, name="ident")
        nc.vector.memset(ident[:], 0.0)
        ones = keep.tile([P, 32], F32, name="ones")
        nc.vector.memset(ones[:], 1.0)
        ramp = keep.tile([P, 32], F32, name="ramp", align_bytes=64)
        nc.vector.tensor_tensor_scan(ramp[:], ones[:], ones[:], 0.0, ALU.mult, ALU.add)
        ramp_t = keep.tile([P, 32], F32, name="ramp_t", align_bytes=64)
        nc.vector.transpose(ramp_t[:], ramp[:])
        for q in range(4):
            quad = slice(32 * q, 32 * q + 32)
            nc.vector.tensor_tensor(ident[quad, quad], ramp[quad, :], ramp_t[quad, :], ALU.is_equal)

        rows = keep.tile([P, P], F32, name="rows")
        nc.gpsimd.memset(rows[:], 0.0)
        before_high = S - 1 + HALF
        nc.sync.dma_start(out=rows[2:5, :], in_=rew.rearrange("r j -> (r j)")[before_high : before_high + 3 * P].rearrange("(c n) -> c n", n=P))
        nc.sync.dma_start(out=rows[0:2, :], in_=gam.rearrange("r j -> (r j)")[before_high : before_high + 2 * P].rearrange("(c n) -> c n", n=P))
        mu_sb = load("mu_sb", mu, [P, S])
        rew_low = load("rew_low", rew[:, 0 : HALF + 3], [P, HALF + 3])
        cap_sb = load("cap_sb", cap, [P, S])
        gam_sb = load("gam_sb", gam, [P, S])

        def row(name, pad=0):
            t = keep.tile([P, S + pad], F32, name=name)
            if pad:
                nc.gpsimd.memset(t[:, S:], 0.0)
            return t

        ex, ratio = row("ex"), row("ratio")
        gc, sa = row("gc", 1), row("sa", 2)
        dlt = keep.tile([P, S + 1], F32, name="dlt")
        nc.scalar.activation(out=dlt[:, S:], in_=gc[:, S:], func=ACT.Copy)
        u, cc2, w, o, res = row("u"), row("cc2"), row("w"), row("o"), row("res")

        def turn(dst, src, start, stop):
            nc.tensor.matmul(dst, lhsT=src, rhs=ident[:], is_transpose=True, start=start, stop=stop)

        picked_scales = keep.tile([P, S], U8, name="picked_scales", align_bytes=64)
        nc.vector.tensor_copy(picked_scales[:], table_scales[:].indirect(offsets[:]))

        def quantise(name, raw):
            grouped = keep.tile([P, M, 4], BF16, name=name + "_grouped", tag=name + "_grouped", align_bytes=64)
            nc.scalar.activation(out=grouped[:], in_=raw[:].rearrange("p j m -> p m j"), func=ACT.Copy)
            codes = keep.tile([P, M], U32, name=name + "_codes", align_bytes=64)
            scales = keep.tile([P, M], U8, name=name + "_scales", align_bytes=64)
            nc.vector.quantize_mx(out=codes[:].bitcast(FP8X4), scales=scales[:], in_=grouped[:].rearrange("p m j -> p (m j)"))
            return codes, scales

        w1_codes, w1_scales = quantise("w1", w1_raw)

        picked_words = [keep.tile([P, HALF], U32, name="picked_words%d" % h, align_bytes=64) for h in range(2)]

        def words_of(c, n=P):
            return picked_words[c // 2][:, (c % 2) * P : (c % 2) * P + n]

        yl = []
        for c in range(CHUNKS):
            nc.vector.tensor_copy(words_of(c), table_words[:].indirect(offsets[:, c * P // 16 : (c + 1) * P // 16]))
            bank = psum.tile([P, P], F32, name="yl%d" % c)
            nc.tensor.matmul_mx(out=bank[:], lhsT=w1_codes[:].bitcast(FP8X4), lhsT_scale=w1_scales[:],
                                rhs=words_of(c).bitcast(FP8X4), rhs_scale=picked_scales[:, c * P : (c + 1) * P], start=True, stop=True)
            yl.append(bank)

        w2_codes, w2_scales = quantise("w2", w2_raw)

        val_low = psum.tile([P, HALF + 64], F32, name="val_low")
        nc.tensor.matmul_mx(out=val_low[:, 0:HALF], lhsT=w2_codes[:].bitcast(FP8X4), lhsT_scale=w2_scales[:],
                            rhs=picked_words[0][:].bitcast(FP8X4), rhs_scale=picked_scales[:, 0:HALF], start=True, stop=True)
        nc.tensor.matmul_mx(out=val_low[:, HALF : HALF + 64], lhsT=w2_codes[:].bitcast(FP8X4), lhsT_scale=w2_scales[:],
                            rhs=words_of(2, 64).bitcast(FP8X4), rhs_scale=picked_scales[:, HALF : HALF + 64], start=True, stop=True)
        val_t = psum.tile([P, 2, M], F32, name="val_t")
        for i in range(2):
            c = 2 + i
            nc.tensor.matmul_mx(out=val_t[:, i, :], lhsT=words_of(c).bitcast(FP8X4), lhsT_scale=picked_scales[:, c * P : (c + 1) * P],
                                rhs=w2_codes[:].bitcast(FP8X4), rhs_scale=w2_scales[:], start=True, stop=True)

        tt = nc.vector.tensor_tensor
        for c in range(CHUNKS):
            cols = slice(c * P, (c + 1) * P)
            diff = keep.tile([P, P], F32, name="diff%d" % c, tag="diff%d" % c)
            tt(diff[:], yl[c][:], mu_sb[:, cols], ALU.subtract)
            nc.scalar.activation(out=ex[:, cols], in_=diff[:], func=ACT.Exp)

        rows_t = psum.tile([P, P], F32, name="rows_t", tag="rows_then_td")
        nc.tensor.transpose(rows_t[:], rows[:], ident[:])
        consts = keep.tile([P, 5], F32, name="consts", tag="diff2")
        nc.scalar.activation(out=consts[:], in_=rows_t[:, 0:5], func=ACT.Copy)

        td = psum.tile([P, 3 * P], F32, name="td", tag="rows_then_td")
        turn(td[:, 2 * P : 3 * P], consts[:, 4:5].to_broadcast([P, M]), True, False)
        for i in range(2):
            ahead = keep.tile([P, M], F32, name="ahead%d" % i)
            nc.scalar.activation(out=ahead[:], in_=val_t[:, i, :], func=ACT.Identity, scale=consts[:, i : i + 1], bias=consts[:, 2 + i : 3 + i])
            turn(td[:, i * P : (i + 1) * P], ahead[:], False, False)
        minus = keep.tile([P, 2, M], F32, name="minus", tag="diff3")
        nc.scalar.activation(out=minus[:], in_=val_t[:], func=ACT.Copy, scale=-1.0)
        for i in range(2):
            turn(td[:, i * P + 1 : (i + 1) * P + 1], minus[:, i, :], False, i == 1)
        minus_val = psum.tile([P, HALF], F32, name="minus_val")
        for i in range(2):
            turn(minus_val[:, i * P : (i + 1) * P], minus[:, i, :], True, True)

        back = keep.tile([P, HALF + 3], F32, name="back")
        nxt = keep.tile([P, HALF + 3], F32, name="nxt")
        td_low = keep.tile([P, HALF + 3], F32, name="td_low")

        def part(t, h, reach=0, by=0):
            return t[:, by : HALF + reach + by] if h == 0 else t[:, HALF + reach + by : S + by]

        steps = {
            "back": lambda h: tt(back[:], rew_low[:], val_low[:, 0 : HALF + 3], ALU.subtract),
            "nxt": lambda h: tt(nxt[:], val_low[:, 1 : HALF + 4], gam_sb[:, 0 : HALF + 3], ALU.mult),
            "td": lambda h: tt(td_low[:], nxt[:], back[:], ALU.add),
            "ratio": lambda h: tt(part(ratio, h), part(ex, h), part(cap_sb, h), ALU.min),
            "gc": lambda h: tt(part(gc, h), part(ratio, h), part(gam_sb, h), ALU.mult),
            "cc2": lambda h: tt(part(cc2, h), part(gc, h), part(gc, h, 0, 1), ALU.mult),
            "dlt": lambda h: tt(part(dlt, h, 3), td[:, 4 : HALF + 1] if h else td_low[:], part(ratio, h, 3), ALU.mult),
            "u": lambda h: tt(part(u, h, 2), part(gc, h, 2), part(dlt, h, 2, 1), ALU.mult),
            "sa": lambda h: tt(part(sa, h, 2), part(dlt, h, 2), part(u, h, 2), ALU.add),
            "w": lambda h: tt(part(w, h), part(cc2, h), part(sa, h, 0, 2), ALU.mult),
            "o": lambda h: tt(part(o, h), part(sa, h), minus_val[:] if h else val_low[:, 0:HALF], ALU.subtract if h else ALU.add),
            "res": lambda h: tt(part(res, h), part(o, h), part(w, h), ALU.add),
        }
        order = [("back", 0), ("ratio", 0), ("ratio", 1), ("nxt", 0), ("gc", 0), ("td", 0), ("gc", 1), ("dlt", 0), ("cc2", 0), ("u", 0),
                 ("dlt", 1), ("sa", 0), ("u", 1), ("w", 0), ("sa", 1), ("o", 0), ("cc2", 1), ("o", 1), ("w", 1), ("res", 0), ("res", 1)]
        for name, h in order:
            steps[name](h)
            if name == "res":
                nc.sync.dma_start(out=part(out, h), in_=part(res, h))
